import numpy as np
import ml_dtypes


def mxq(x, axis, fmt="e4m3"):
    dtype, down = {"e4m3": (ml_dtypes.float8_e4m3fn, 7), "e5m2": (ml_dtypes.float8_e5m2, 14)}[fmt]
    v = np.moveaxis(np.asarray(x, np.float32).astype(ml_dtypes.bfloat16).astype(np.float64), axis, -1)
    blocks = v.reshape(v.shape[:-1] + (-1, 32))
    amax = np.abs(blocks).max(-1, keepdims=True)
    byte = np.maximum(np.where(amax > 0, np.frexp(amax)[1] - 1 + 127, 0) - down, 1)
    scale = np.exp2(byte - 127.0)
    codes = (blocks / scale).astype(np.float32).astype(dtype).astype(np.float64)
    return np.moveaxis((codes * scale).reshape(v.shape), -1, axis)


WIDE = False


def mx_kscale(k):
    if not WIDE:
        return np.ones(k)
    levels = np.array([10, -10, 5, -5, 0])
    if k % 512:
        return np.exp2(np.random.permutation(np.resize(levels, k // 32))).repeat(32)
    a = np.empty((k // 512, 16))
    for p in range(k // 512):
        a[p, :8] = np.random.permutation(np.resize(levels, 8))
        for g in range(8):
            far = levels[np.abs(levels - a[p, g]) >= 10]
            a[p, g + 8] = far[np.random.randint(len(far))]
    return np.exp2(a.ravel()).repeat(32)


def f64(x):
    return np.asarray(x).astype(np.float64)


def striped(idx):
    return np.tile(idx.reshape(-1, 16).T, (8, 1)).astype(np.uint16)


def unstriped(offs):
    return offs[:16].T.reshape(-1).astype(np.int64)


def striped8(idx):
    return np.concatenate([x.reshape(-1, 16).T for x in idx]).astype(np.uint16)


def runs(offs, k):
    lists = np.stack([offs[16 * r : 16 * r + 16].T.reshape(-1) for r in range(8)]).astype(np.int64)
    return lists[np.arange(k) % 512 // 64]


def pack_weight(w):
    k, n = w.shape
    w = f64(np.asarray(w, np.float32).astype(ml_dtypes.bfloat16)).reshape(k // 32, 32, n)
    amax = np.abs(w).max(1)
    byte = np.clip(np.where(amax > 0, np.frexp(amax)[1] - 1 + 127 - 7, 1), 1, 254)
    scaled = (w * np.exp2(127.0 - byte)[:, None, :]).reshape(k, n).astype(np.float32)
    words = np.ascontiguousarray(scaled.reshape(k // 512, 128, 4, n).transpose(0, 1, 3, 2)).astype(ml_dtypes.float8_e4m3fn).view(np.uint8)
    return words, np.ascontiguousarray(byte.astype(np.uint8).reshape(k // 512, 16, n))


def unpack_weight(words, scales):
    g, p, n, _ = words.shape
    vals = np.ascontiguousarray(words).view(ml_dtypes.float8_e4m3fn).astype(np.float64) * np.repeat(np.exp2(scales.astype(np.float64) - 127.0), 8, axis=1)[..., None]
    return vals.transpose(0, 1, 3, 2).reshape(g * 512, n)

def planes(y):
    n, m = y.shape
    v = y.astype(np.float32).astype(ml_dtypes.bfloat16).astype(np.float64).reshape(n // 32, 32, m)
    top = np.abs(v).max(1)
    byte = np.clip(np.where(top > 0, np.frexp(top)[1] - 1 + 127 - 7, 1), 1, 254)
    codes = (v * np.exp2(127.0 - byte)[:, None, :]).reshape(n, m).astype(np.float32).astype(ml_dtypes.float8_e4m3fn).view(np.uint8)
    words = codes.reshape(n // 512, 128, 4, m).transpose(0, 1, 3, 2)
    return np.ascontiguousarray(words), np.ascontiguousarray(byte.astype(np.uint8).reshape(n // 512, 16, m))


K, T, S, N, H = 512, 2048, 512, 512, 512


def setup_inputs():
    n = np.random.standard_normal
    s = mx_kscale(K)[:, None]
    u = mx_kscale(H)
    packed_xT = pack_weight(n((K, T)) * s)
    packed_w1 = pack_weight(n((K, H)) / np.sqrt(K) / s)
    packed_w2 = pack_weight(n((K, H)) / np.sqrt(K) / s)
    packed_w3 = pack_weight(n((K, H)) / np.sqrt(K) / s)
    packed_w4 = pack_weight(n((H, N)) / np.sqrt(H) / u[:, None])
    return {
        "x_words": packed_xT[0],
        "x_scales": packed_xT[1],
        "w1_words": packed_w1[0],
        "w1_scales": packed_w1[1],
        "w2_words": packed_w2[0],
        "w2_scales": packed_w2[1],
        "w3_words": packed_w3[0],
        "w3_scales": packed_w3[1],
        "gn": (np.random.uniform(0.5, 1.5, (H, 1)) * u[:, None]).astype(np.float32),
        "w4_words": packed_w4[0],
        "w4_scales": packed_w4[1],
        "offs": striped(np.random.permutation(T)[:S]),
        "two": striped(np.random.permutation(T)[:S]),
        "three": striped(np.random.permutation(T)[:S]),
        "n1": striped8(np.stack([np.random.permutation(S) for _ in range(8)])),
        "n2": striped8(np.stack([np.random.permutation(S) for _ in range(8)])),
        "n3": striped8(np.stack([np.random.permutation(S) for _ in range(8)])),
        "n4": striped8(np.stack([np.random.permutation(S) for _ in range(8)])),
        "n5": striped8(np.stack([np.random.permutation(S) for _ in range(8)])),
        "n6": striped8(np.stack([np.random.permutation(S) for _ in range(8)])),
        "n7": striped8(np.stack([np.random.permutation(S) for _ in range(8)])),
        "n8": striped8(np.stack([np.random.permutation(S) for _ in range(8)])),
    }


def reference(x_words, x_scales, w1_words, w1_scales, w2_words, w2_scales, w3_words, w3_scales, gn, w4_words, w4_scales, offs, two, three, n1, n2, n3, n4, n5, n6, n7, n8):
    xq = unpack_weight(x_words, x_scales)[:, unstriped(offs)]
    y = unpack_weight(w1_words, w1_scales).T @ xq
    x_two = unpack_weight(x_words, x_scales)[:, unstriped(two)]
    d = unpack_weight(w2_words, w2_scales).T @ x_two
    m1 = np.maximum(y[np.arange(H)[:, None], runs(n1, H)] + d[np.arange(H)[:, None], runs(n3, H)], y[np.arange(H)[:, None], runs(n2, H)] + d[np.arange(H)[:, None], runs(n4, H)])
    x_three = unpack_weight(x_words, x_scales)[:, unstriped(three)]
    b = unpack_weight(w3_words, w3_scales).T @ x_three
    z = f64(gn) * ((m1 - (m1[np.arange(H)[:, None], runs(n5, H)])) / (np.abs(b) + np.abs(b[np.arange(H)[:, None], runs(n6, H)]) + 0.5))
    h = unpack_weight(w4_words, w4_scales).T @ mxq(z, 0, "e4m3")
    out_0 = np.maximum(h[np.arange(N)[:, None], runs(n7, N)], h[np.arange(N)[:, None], runs(n8, N)]) - (0.75 * h)
    return (out_0,) + planes(out_0)

@@ -1,0 +1,278 @@
+from contextlib import ExitStack
+
+import concourse.mybir as mybir
+
+K, T, S, N, H = 512, 2048, 512, 512, 512
+FLOPS = 4 * 2 * 512 * 512 * 512
+
+F32 = mybir.dt.float32
+BF16 = mybir.dt.bfloat16
+I32 = mybir.dt.int32
+U32 = mybir.dt.uint32
+U16 = mybir.dt.uint16
+U8 = mybir.dt.uint8
+FP8X4 = mybir.dt.float8_e4m3fn_x4
+ALU = mybir.AluOpType
+ACT = mybir.ActivationFunctionType
+
+P = 128
+PACK = 4
+LIST_COLS = S // 16
+WIDE = 2 * S
+CHUNKS = ((0, 256), (256, 384), (384, 512))
+
+
+def tile_picked_triopathbnormbover_none_po_kernel(
+    tc, x_words, x_scales, w1_words, w1_scales, w2_words, w2_scales, w3_words, w3_scales, gn,
+    w4_words, w4_scales, offs, two, three, n1, n2, n3, n4, n5, n6, n7, n8, out_0, out_1, out_2,
+):
+    nc = tc.nc
+    with ExitStack() as ctx:
+        keep = ctx.enter_context(tc.tile_pool(name="keep", bufs=1))
+        psum = ctx.enter_context(tc.psum_pool(name="psum", bufs=8))
+
+        def sb(name, shape, dtype):
+            return keep.tile(shape, dtype, name=name, align_bytes=64)
+
+        def bank():
+            return psum.tile([P, S], F32, name="bank")
+
+        def words_view(ap):
+            return ap[0].rearrange("p n t -> p (n t)").bitcast(I32)
+
+        def load_list(name, ap):
+            tile = keep.tile([P, LIST_COLS], U16, name=name)
+            nc.sync.dma_start(tile[:], ap)
+            return tile
+
+        def load_scales(plane, first_row, cols, ap):
+            for q in range(4):
+                rows = slice(32 * q + first_row, 32 * q + first_row + 4)
+                nc.sync.dma_start(plane[:].bitcast(I32)[rows, cols], ap[0, 4 * q : 4 * q + 4, :].bitcast(I32))
+
+        def load_words(name, ap, width):
+            tile = sb(name, [P, width], I32)
+            nc.sync.dma_start(tile[:], words_view(ap))
+            return tile
+
+        x_plane = sb("x_plane", [P, T], U8)
+        nc.vector.memset(x_plane[:].bitcast(I32), 0)
+        w_planes = [sb("w_plane_a", [P, H], U8), sb("w_plane_b", [P, H], U8)]
+        for plane in w_planes:
+            nc.vector.memset(plane[:].bitcast(I32), 0)
+        half = keep.tile([P, 1], F32, name="half")
+        nc.vector.memset(half[:], 0.5)
+
+        load_scales(x_plane, 0, slice(0, T // 4), x_scales)
+        token_lists = [load_list("offs", offs), load_list("two", two), load_list("three", three)]
+        x_codes = load_words("x_codes", x_words, T)
+        all_cols = slice(0, H // 4)
+        w1_raw = load_words("w1_raw", w1_words, H)
+        load_scales(w_planes[0], 0, all_cols, w1_scales)
+        w2_raw = load_words("w2_raw", w2_words, H)
+        load_scales(w_planes[0], 4, all_cols, w2_scales)
+        l1, l2, l3, l4 = (load_list(name, ap) for name, ap in (("n1", n1), ("n2", n2), ("n3", n3), ("n4", n4)))
+        w3_raw = load_words("w3_raw", w3_words, H)
+        load_scales(w_planes[1], 0, all_cols, w3_scales)
+        load_scales(w_planes[1], 4, all_cols, w4_scales)
+        l6 = load_list("n6", n6)
+        gain = keep.tile([P, PACK], F32, name="gain")
+        nc.sync.dma_start(gain[:], gn.rearrange("(p t) o -> p (t o)", t=PACK))
+        l5 = load_list("n5", n5)
+        w4_raw = load_words("w4_raw", w4_words, N)
+        l7, l8 = load_list("n7", n7), load_list("n8", n8)
+
+        def deal_words(name, raw):
+            dealt = sb(name, [P, H], I32)
+            nc.vector.tensor_copy(
+                dealt[:].rearrange("p (t b i) -> p b t i", t=PACK, i=4),
+                raw[:].rearrange("p (b i t) -> p b t i", t=PACK, i=4),
+            )
+            return dealt
+
+        def deal_scales(name, plane):
+            dealt = sb(name, [P, H], U8)
+            nc.vector.tensor_copy(
+                dealt[:].rearrange("p (t b i) -> p b t i", t=PACK, i=16),
+                plane[:].rearrange("p (b i t) -> p b t i", t=PACK, i=16),
+            )
+            return dealt
+
+        def pick_scales(i):
+            picked = sb(f"picked_scales{i}", [P, S], U8)
+            nc.vector.tensor_copy(picked[:], x_plane[:].indirect(token_lists[i][:]))
+            return picked
+
+        def pick_words(i):
+            picked = sb(f"picked_words{i}", [P, S], U32)
+            nc.vector.tensor_copy(picked[:], x_codes[:].bitcast(U32).indirect(token_lists[i][:]))
+            return picked
+
+        def product(out, w_dealt, w_plane, first_row, t, codes, scales):
+            cols = slice(P * t, P * (t + 1))
+            nc.tensor.matmul_mx(
+                out=out, lhsT=w_dealt[:, cols].bitcast(FP8X4), lhsT_scale=w_plane[first_row:P, cols],
+                rhs=codes.bitcast(FP8X4), rhs_scale=scales, start=True, stop=True,
+            )
+
+        tok_scales = [pick_scales(i) for i in range(3)]
+        tok_words = [pick_words(0)]
+        w1_dealt = deal_words("w1_dealt", w1_raw)
+        tok_words.append(pick_words(1))
+        w2_dealt = deal_words("w2_dealt", w2_raw)
+        plane_a = deal_scales("plane_a", w_planes[0])
+        tok_words.append(pick_words(2))
+
+        y_win, d_win, b_win, b_abs = {}, {}, {}, {}
+
+        def project_yd(t):
+            for win, name, dealt, row, i in ((y_win, "y", w1_dealt, 0, 0), (d_win, "d", w2_dealt, 4, 1)):
+                acc = bank()
+                product(acc[:], dealt, plane_a, row, t, tok_words[i][:], tok_scales[i][:])
+                win[t] = sb(f"{name}_win{t}", [P, WIDE], F32)
+                nc.scalar.copy(win[t][:, 0:S], acc[:])
+
+        def project_b(t):
+            acc = bank()
+            product(acc[:], w3_dealt, plane_b, 0, t, tok_words[2][:], tok_scales[2][:])
+            b_win[t] = sb(f"b_win{t}", [P, WIDE], F32)
+            nc.scalar.activation(b_win[t][:, 0:S], acc[:], ACT.Abs)
+            b_abs[t] = sb(f"b_abs{t}", [P, S], F32)
+            nc.scalar.activation(b_abs[t][:], acc[:], ACT.Abs)
+
+        fetched, sums, m1, m1_neg = {}, {}, {}, {}
+
+        def fetch_y(t, u):
+            fetched[t, u] = sb(f"fetched{t}_{u}", [P, S], F32)
+            nc.vector.tensor_copy(fetched[t, u][:], y_win[t][:].indirect((l1, l2)[u][:]))
+
+        def add_d(t, u):
+            sums[t, u] = sb(f"sums{t}_{u}", [P, S], F32)
+            nc.vector.tensor_tensor(sums[t, u][:], d_win[t][:].indirect((l3, l4)[u][:]), fetched[t, u][:], ALU.add)
+
+        def larger(t):
+            m1[t] = sb(f"m1_{t}", [P, S], F32)
+            nc.vector.tensor_tensor(m1[t][:], sums[t, 0][:], sums[t, 1][:], ALU.max)
+            m1_neg[t] = sb(f"m1_neg{t}", [P, S], F32)
+            nc.scalar.activation(m1_neg[t][:], m1[t][:], ACT.Copy, scale=-1.0)
+
+        denom = sb("denom", [P, PACK, S], F32)
+        logs = sb("logs", [P, PACK, S], F32)
+        recip = sb("recip", [P, PACK, S], F32)
+        factor = sb("factor", [P, PACK, S], F32)
+
+        project_yd(0)
+        project_yd(1)
+        fetch_y(0, 0)
+        fetch_y(0, 1)
+        w3_dealt = deal_words("w3_dealt", w3_raw)
+        plane_b = deal_scales("plane_b", w_planes[1])
+        for t in range(PACK):
+            project_b(t)
+        project_yd(2)
+        project_yd(3)
+        add_d(0, 0)
+        add_d(0, 1)
+        for t in range(1, PACK):
+            fetch_y(t, 0)
+            larger(t - 1)
+            fetch_y(t, 1)
+            add_d(t, 0)
+            add_d(t, 1)
+            if t == 1:
+                for u in range(PACK):
+                    nc.vector.tensor_tensor(denom[:, u, :], b_win[u][:].indirect(l6[:]), b_abs[u][:], ALU.add)
+                for u in range(PACK):
+                    nc.scalar.activation(logs[:, u, :], denom[:, u, :], ACT.Ln, bias=half[:])
+                for u in range(PACK):
+                    nc.scalar.activation(recip[:, u, :], logs[:, u, :], ACT.Exp, scale=-1.0)
+                    nc.scalar.activation(factor[:, u, :], recip[:, u, :], ACT.Copy, scale=gain[:, u : u + 1])
+        w4_dealt = deal_words("w4_dealt", w4_raw)
+        larger(PACK - 1)
+
+        def list_cols(c):
+            return slice(CHUNKS[c][0] // 16, CHUNKS[c][1] // 16)
+
+        def width(c):
+            return CHUNKS[c][1] - CHUNKS[c][0]
+
+        def cols(c):
+            return slice(*CHUNKS[c])
+
+        def by_row(ap):
+            return ap.rearrange("p t (c i) -> p c t i", i=2)
+
+        def woven(ap):
+            return ap.rearrange("p (c i t) -> p c t i", i=2, t=PACK)
+
+        diff = [sb(f"diff{c}", [P, PACK, width(c)], F32) for c in range(3)]
+        z_bf = [sb(f"z_bf{c}", [P, PACK * width(c)], BF16) for c in range(3)]
+        z_codes = [sb(f"z_codes{c}", [P, width(c)], U32) for c in range(3)]
+        z_scales = [sb(f"z_scales{c}", [P, width(c)], U8) for c in range(3)]
+        h_win = [sb(f"h_win{t}", [P, S], F32) for t in range(PACK)]
+        h_part = [sb(f"h_part{c}", [P, PACK, width(c)], F32) for c in range(3)]
+
+        def fetch_m1(c, t):
+            nc.vector.tensor_tensor(diff[c][:, t, :], m1_neg[t][:].indirect(l5[:, list_cols(c)]), m1[t][:, cols(c)], ALU.add)
+
+        def make_z(c):
+            nc.vector.tensor_tensor(woven(z_bf[c][:]), by_row(diff[c][:]), by_row(factor[:, :, cols(c)]), ALU.mult)
+
+        def last_product(c):
+            nc.vector.quantize_mx(out=z_codes[c][:].bitcast(FP8X4), scales=z_scales[c][:], in_=z_bf[c][:])
+            accs = []
+            for t in range(PACK):
+                acc = bank()
+                product(acc[:, 0 : width(c)], w4_dealt, plane_b, 4, t, z_codes[c][:], z_scales[c][:])
+                nc.scalar.copy(h_win[t][:, cols(c)], acc[:, 0 : width(c)])
+                accs.append(acc)
+            for t in range(PACK):
+                nc.scalar.activation(h_part[c][:, t, :], accs[t][:, 0 : width(c)], ACT.Copy, scale=-0.75)
+
+        for t in range(PACK):
+            fetch_m1(0, t)
+        for c in (1, 2):
+            fetch_m1(c, 0)
+            make_z(c - 1)
+            fetch_m1(c, 1)
+            last_product(c - 1)
+            fetch_m1(c, 2)
+            fetch_m1(c, 3)
+        make_z(2)
+        last_product(2)
+
+        cand = [[sb(f"cand{c}_{u}", [P, PACK, width(c)], F32) for u in range(2)] for c in range(3)]
+        result = [sb(f"result{c}", [P, PACK, width(c)], F32) for c in range(3)]
+        result_bf = [sb(f"result_bf{c}", [P, PACK * width(c)], BF16) for c in range(3)]
+        out_codes = sb("out_codes", [P, S], U32)
+        out_plane = sb("out_plane", [P, S], U8)
+        out_rows = out_0.rearrange("(p t) j -> p t j", t=PACK)
+
+        def fetch_h(c, t):
+            for u, lst in enumerate((l7, l8)):
+                nc.vector.tensor_tensor(cand[c][u][:, t, :], h_win[t][:].indirect(lst[:, list_cols(c)]), h_part[c][:, t, :], ALU.add)
+
+        def finish(c):
+            nc.vector.tensor_tensor(result[c][:], cand[c][0][:], cand[c][1][:], ALU.max)
+            nc.sync.dma_start(out_rows[:, :, cols(c)], result[c][:])
+
+        def planes(c):
+            nc.vector.quantize_mx(out=out_codes[:, cols(c)].bitcast(FP8X4), scales=out_plane[:, cols(c)], in_=result_bf[c][:])
+            nc.sync.dma_start(words_view(out_1)[:, cols(c)], out_codes[:, cols(c)].bitcast(I32))
+
+        for t in range(PACK):
+            fetch_h(0, t)
+        for c in (1, 2):
+            fetch_h(c, 0)
+            finish(c - 1)
+            nc.scalar.copy(woven(result_bf[c - 1][:]), by_row(result[c - 1][:]))
+            fetch_h(c, 1)
+            fetch_h(c, 2)
+            fetch_h(c, 3)
+            planes(c - 1)
+        nc.vector.tensor_tensor(woven(result_bf[2][:]), by_row(cand[2][0][:]), by_row(cand[2][1][:]), ALU.max)
+        finish(2)
+        planes(2)
+        for q in range(4):
+            queue = nc.scalar if q % 2 else nc.sync
+            queue.dma_start(out_2[0, 4 * q : 4 * q + 4, :].bitcast(I32), out_plane[:].bitcast(I32)[32 * q : 32 * q + 4, :])

@@ -1,6 +1,7 @@
 from contextlib import ExitStack
 
 import concourse.mybir as mybir
+from concourse.masks import make_identity
 
 K, T, S, N, H = 512, 2048, 512, 512, 512
 FLOPS = 4 * 2 * 512 * 512 * 512
@@ -29,10 +30,11 @@ def tile_picked_triopathbnormbover_none_po_kernel(
     nc = tc.nc
     with ExitStack() as ctx:
         keep = ctx.enter_context(tc.tile_pool(name="keep", bufs=1))
+        ring = ctx.enter_context(tc.tile_pool(name="ring", bufs=4))
         psum = ctx.enter_context(tc.psum_pool(name="psum", bufs=8))
 
-        def sb(name, shape, dtype):
-            return keep.tile(shape, dtype, name=name, align_bytes=64)
+        def sb(name, shape, dtype, tag=None):
+            return keep.tile(shape, dtype, name=name, tag=tag or name, align_bytes=64)
 
         def bank():
             return psum.tile([P, S], F32, name="bank")
@@ -56,26 +58,32 @@ def tile_picked_triopathbnormbover_none_po_kernel(
             return tile
 
         x_plane = sb("x_plane", [P, T], U8)
-        nc.vector.memset(x_plane[:].bitcast(I32), 0)
+        nc.vector.memset(x_plane[:].bitcast(I32)[:, 0 : T // 8], 0)
+        nc.gpsimd.memset(x_plane[:].bitcast(I32)[:, T // 8 : T // 4], 0)
         w_planes = [sb("w_plane_a", [P, H], U8), sb("w_plane_b", [P, H], U8)]
         for plane in w_planes:
             nc.vector.memset(plane[:].bitcast(I32), 0)
         half = keep.tile([P, 1], F32, name="half")
         nc.vector.memset(half[:], 0.5)
+        warm = keep.tile([P, 1], F32, name="warm")
+        nc.scalar.activation(warm[:], half[:], ACT.Ln, bias=half[:])
+
+        identity = sb("identity", [P, P], F32)
+        make_identity(nc, identity[:])
 
         load_scales(x_plane, 0, slice(0, T // 4), x_scales)
-        token_lists = [load_list("offs", offs), load_list("two", two), load_list("three", three)]
+        tok_three, tok_offs, tok_two = load_list("three", three), load_list("offs", offs), load_list("two", two)
+        token_lists = [tok_offs, tok_two, tok_three]
         x_codes = load_words("x_codes", x_words, T)
         all_cols = slice(0, H // 4)
-        w1_raw = load_words("w1_raw", w1_words, H)
-        load_scales(w_planes[0], 0, all_cols, w1_scales)
-        w2_raw = load_words("w2_raw", w2_words, H)
-        load_scales(w_planes[0], 4, all_cols, w2_scales)
-        l1, l2, l3, l4 = (load_list(name, ap) for name, ap in (("n1", n1), ("n2", n2), ("n3", n3), ("n4", n4)))
+        load_scales(w_planes[0], 0, all_cols, w3_scales)
         w3_raw = load_words("w3_raw", w3_words, H)
-        load_scales(w_planes[1], 0, all_cols, w3_scales)
+        load_scales(w_planes[0], 4, all_cols, w1_scales)
+        w1_raw = load_words("w1_raw", w1_words, H)
+        load_scales(w_planes[1], 0, all_cols, w2_scales)
+        w2_raw = load_words("w2_raw", w2_words, H)
         load_scales(w_planes[1], 4, all_cols, w4_scales)
-        l6 = load_list("n6", n6)
+        l1, l2, l3, l4, l6 = (load_list(name, ap) for name, ap in (("n1", n1), ("n2", n2), ("n3", n3), ("n4", n4), ("n6", n6)))
         gain = keep.tile([P, PACK], F32, name="gain")
         nc.sync.dma_start(gain[:], gn.rearrange("(p t) o -> p (t o)", t=PACK))
         l5 = load_list("n5", n5)
@@ -103,8 +111,8 @@ def tile_picked_triopathbnormbover_none_po_kernel(
             nc.vector.tensor_copy(picked[:], x_plane[:].indirect(token_lists[i][:]))
             return picked
 
-        def pick_words(i):
-            picked = sb(f"picked_words{i}", [P, S], U32)
+        def pick_words(i, tag=None):
+            picked = sb(f"picked_words{i}", [P, S], U32, tag)
             nc.vector.tensor_copy(picked[:], x_codes[:].bitcast(U32).indirect(token_lists[i][:]))
             return picked
 
@@ -115,62 +123,104 @@ def tile_picked_triopathbnormbover_none_po_kernel(
                 rhs=codes.bitcast(FP8X4), rhs_scale=scales, start=True, stop=True,
             )
 
-        tok_scales = [pick_scales(i) for i in range(3)]
-        tok_words = [pick_words(0)]
-        w1_dealt = deal_words("w1_dealt", w1_raw)
-        tok_words.append(pick_words(1))
-        w2_dealt = deal_words("w2_dealt", w2_raw)
-        plane_a = deal_scales("plane_a", w_planes[0])
-        tok_words.append(pick_words(2))
+        tok_scales, tok_words = {}, {}
+        y_win, d_win, b_abs, b_log, b_far = {}, {}, {}, {}, {}
 
-        y_win, d_win, b_win, b_abs = {}, {}, {}, {}
+        def project_y(t):
+            acc = bank()
+            product(acc[:], w1_dealt, plane_a, 4, t, tok_words[0][:], tok_scales[0][:])
+            y_win[t] = sb(f"y_win{t}", [P, WIDE], F32)
+            nc.scalar.copy(y_win[t][:, 0:S], acc[:])
 
-        def project_yd(t):
-            for win, name, dealt, row, i in ((y_win, "y", w1_dealt, 0, 0), (d_win, "d", w2_dealt, 4, 1)):
-                acc = bank()
-                product(acc[:], dealt, plane_a, row, t, tok_words[i][:], tok_scales[i][:])
-                win[t] = sb(f"{name}_win{t}", [P, WIDE], F32)
-                nc.scalar.copy(win[t][:, 0:S], acc[:])
+        def project_d(t):
+            acc = bank()
+            product(acc[:], w2_dealt, plane_b, 0, t, tok_words[1][:], tok_scales[1][:])
+            d_win[t] = sb(f"d_win{t}", [P, WIDE], F32)
+            nc.scalar.copy(d_win[t][:, 0:S], acc[:])
 
         def project_b(t):
             acc = bank()
-            product(acc[:], w3_dealt, plane_b, 0, t, tok_words[2][:], tok_scales[2][:])
-            b_win[t] = sb(f"b_win{t}", [P, WIDE], F32)
-            nc.scalar.activation(b_win[t][:, 0:S], acc[:], ACT.Abs)
+            product(acc[:], w3_dealt, plane_a, 0, t, tok_words[2][:], tok_scales[2][:])
             b_abs[t] = sb(f"b_abs{t}", [P, S], F32)
             nc.scalar.activation(b_abs[t][:], acc[:], ACT.Abs)
+
+        def log_b(t):
+            b_log[t] = sb(f"b_log{t}", [P, WIDE], F32)
+            nc.scalar.activation(b_log[t][:, 0:S], b_abs[t][:], ACT.Ln, bias=half[:])
+
+        def fetch_b(t):
+            b_far[t] = sb(f"b_far{t}", [P, S], F32)
+            nc.scalar.activation(b_far[t][:], b_log[t][:].indirect(l6[:]), ACT.Exp)
+
+        logs, recips, factor = {}, {}, {}
+
+        def log_denominator(jb):
+            acc = bank()
+            for t in range(PACK):
+                for term, first in ((b_far[t], True), (b_abs[t], False)):
+                    nc.tensor.matmul(acc[:, P * t : P * (t + 1)], lhsT=term[:, P * jb : P * (jb + 1)], rhs=identity[:],
+                                     is_transpose=True, start=first, stop=not first)
+            logs[jb] = sb(f"logs{jb}", [P, S], F32)
+            nc.scalar.activation(logs[jb][:], acc[:], ACT.Ln)
+
+        def reciprocal(jb):
+            recips[jb] = sb(f"recips{jb}", [P, S], F32)
+            nc.scalar.activation(recips[jb][:], logs[jb][:], ACT.Exp, scale=-1.0)
+            factor[jb] = bank()
+            for t in range(PACK):
+                nc.tensor.transpose(factor[jb][:, P * t : P * (t + 1)], recips[jb][:, P * t : P * (t + 1)], identity[:])
 
         fetched, sums, m1, m1_neg = {}, {}, {}, {}
 
         def fetch_y(t, u):
-            fetched[t, u] = sb(f"fetched{t}_{u}", [P, S], F32)
+            fetched[t, u] = ring.tile([P, S], F32, name="fetched")
             nc.vector.tensor_copy(fetched[t, u][:], y_win[t][:].indirect((l1, l2)[u][:]))
 
         def add_d(t, u):
-            sums[t, u] = sb(f"sums{t}_{u}", [P, S], F32)
+            sums[t, u] = ring.tile([P, S], F32, name="sums")
             nc.vector.tensor_tensor(sums[t, u][:], d_win[t][:].indirect((l3, l4)[u][:]), fetched[t, u][:], ALU.add)
 
+        m1_raw = {}
+
         def larger(t):
-            m1[t] = sb(f"m1_{t}", [P, S], F32)
-            nc.vector.tensor_tensor(m1[t][:], sums[t, 0][:], sums[t, 1][:], ALU.max)
+            m1_raw[t] = sb(f"m1_raw{t}", [P, S], F32)
+            nc.vector.tensor_tensor(m1_raw[t][:], sums[t, 0][:], sums[t, 1][:], ALU.max)
+
+        def gained(t):
+            raw = m1_raw[t]
             m1_neg[t] = sb(f"m1_neg{t}", [P, S], F32)
-            nc.scalar.activation(m1_neg[t][:], m1[t][:], ACT.Copy, scale=-1.0)
+            nc.scalar.activation(m1_neg[t][:], raw[:], ACT.Copy, scale=gain_neg[:, t : t + 1])
+            m1[t] = sb(f"m1_{t}", [P, S], F32)
+            nc.scalar.activation(m1[t][:], raw[:], ACT.Copy, scale=gain[:, t : t + 1])
 
-        denom = sb("denom", [P, PACK, S], F32)
-        logs = sb("logs", [P, PACK, S], F32)
-        recip = sb("recip", [P, PACK, S], F32)
-        factor = sb("factor", [P, PACK, S], F32)
-
-        project_yd(0)
-        project_yd(1)
-        fetch_y(0, 0)
-        fetch_y(0, 1)
+        for i in (2, 0, 1):
+            tok_scales[i] = pick_scales(i)
+        tok_words[2] = pick_words(2)
         w3_dealt = deal_words("w3_dealt", w3_raw)
-        plane_b = deal_scales("plane_b", w_planes[1])
+        plane_a = deal_scales("plane_a", w_planes[0])
         for t in range(PACK):
             project_b(t)
-        project_yd(2)
-        project_yd(3)
+        tok_words[0] = pick_words(0, "w_plane_a")
+        w1_dealt = deal_words("w1_dealt", w1_raw)
+        tok_words[1] = pick_words(1, "w1_raw")
+        w2_dealt = deal_words("w2_dealt", w2_raw)
+        plane_b = deal_scales("plane_b", w_planes[1])
+        project_y(0)
+        project_y(1)
+        project_d(0)
+        for t in range(PACK):
+            log_b(t)
+        project_d(1)
+        project_y(2)
+        project_d(2)
+        for t in range(PACK):
+            fetch_b(t)
+        project_y(3)
+        project_d(3)
+        gain_neg = keep.tile([P, PACK], F32, name="gain_neg")
+        nc.scalar.activation(gain_neg[:], gain[:], ACT.Copy, scale=-1.0)
+        fetch_y(0, 0)
+        fetch_y(0, 1)
         add_d(0, 0)
         add_d(0, 1)
         for t in range(1, PACK):
@@ -179,16 +229,18 @@ def tile_picked_triopathbnormbover_none_po_kernel(
             fetch_y(t, 1)
             add_d(t, 0)
             add_d(t, 1)
-            if t == 1:
-                for u in range(PACK):
-                    nc.vector.tensor_tensor(denom[:, u, :], b_win[u][:].indirect(l6[:]), b_abs[u][:], ALU.add)
-                for u in range(PACK):
-                    nc.scalar.activation(logs[:, u, :], denom[:, u, :], ACT.Ln, bias=half[:])
-                for u in range(PACK):
-                    nc.scalar.activation(recip[:, u, :], logs[:, u, :], ACT.Exp, scale=-1.0)
-                    nc.scalar.activation(factor[:, u, :], recip[:, u, :], ACT.Copy, scale=gain[:, u : u + 1])
         w4_dealt = deal_words("w4_dealt", w4_raw)
         larger(PACK - 1)
+        gained(0)
+        for jb in range(PACK):
+            log_denominator(jb)
+        gained(1)
+        reciprocal(0)
+        reciprocal(1)
+        gained(2)
+        gained(3)
+        reciprocal(2)
+        reciprocal(3)
 
         def list_cols(c):
             return slice(CHUNKS[c][0] // 16, CHUNKS[c][1] // 16)
@@ -216,7 +268,12 @@ def tile_picked_triopathbnormbover_none_po_kernel(
             nc.vector.tensor_tensor(diff[c][:, t, :], m1_neg[t][:].indirect(l5[:, list_cols(c)]), m1[t][:, cols(c)], ALU.add)
 
         def make_z(c):
-            nc.vector.tensor_tensor(woven(z_bf[c][:]), by_row(diff[c][:]), by_row(factor[:, :, cols(c)]), ALU.mult)
+            for first in range(0, width(c), P):
+                jb = (CHUNKS[c][0] + first) // P
+                nc.vector.tensor_tensor(
+                    woven(z_bf[c][:, PACK * first : PACK * (first + P)]), by_row(diff[c][:, :, first : first + P]),
+                    by_row(factor[jb][:].rearrange("p (t j) -> p t j", t=PACK)), ALU.mult,
+                )
 
         def last_product(c):
             nc.vector.quantize_mx(out=z_codes[c][:].bitcast(FP8X4), scales=z_scales[c][:], in_=z_bf[c][:])
@@ -243,7 +300,7 @@ def tile_picked_triopathbnormbover_none_po_kernel(
 
         cand = [[sb(f"cand{c}_{u}", [P, PACK, width(c)], F32) for u in range(2)] for c in range(3)]
         result = [sb(f"result{c}", [P, PACK, width(c)], F32) for c in range(3)]
-        result_bf = [sb(f"result_bf{c}", [P, PACK * width(c)], BF16) for c in range(3)]
+        result_bf = {c: sb(f"result_bf{c}", [P, PACK * width(c)], BF16) for c in range(2)}
         out_codes = sb("out_codes", [P, S], U32)
         out_plane = sb("out_plane", [P, S], U8)
         out_rows = out_0.rearrange("(p t) j -> p t j", t=PACK)
@@ -260,17 +317,50 @@ def tile_picked_triopathbnormbover_none_po_kernel(
             nc.vector.quantize_mx(out=out_codes[:, cols(c)].bitcast(FP8X4), scales=out_plane[:, cols(c)], in_=result_bf[c][:])
             nc.sync.dma_start(words_view(out_1)[:, cols(c)], out_codes[:, cols(c)].bitcast(I32))
 
+        first, lead = cand[0]
         for t in range(PACK):
-            fetch_h(0, t)
-        for c in (1, 2):
-            fetch_h(c, 0)
-            finish(c - 1)
-            nc.scalar.copy(woven(result_bf[c - 1][:]), by_row(result[c - 1][:]))
-            fetch_h(c, 1)
-            fetch_h(c, 2)
-            fetch_h(c, 3)
-            planes(c - 1)
+            nc.vector.tensor_copy(first[:, t, :], h_win[t][:].indirect(l7[:, list_cols(0)]))
+        for t in range(PACK):
+            nc.vector.tensor_tensor(lead[:, t, :], h_win[t][:].indirect(l8[:, list_cols(0)]), first[:, t, :], ALU.subtract)
+        base, gap = {}, {}
+        for jb in range(2):
+            block = slice(P * jb, P * (jb + 1))
+            acc = bank()
+            for t in range(PACK):
+                for n, term in enumerate((h_part[0], first)):
+                    nc.tensor.matmul(acc[:, P * t : P * (t + 1)], lhsT=term[:, t, block], rhs=identity[:],
+                                     is_transpose=True, start=n == 0, stop=n == 1)
+            base[jb] = sb(f"base{jb}", [P, S], F32)
+            nc.scalar.copy(base[jb][:], acc[:])
+        accs = [bank(), bank()]
+        for t in range(PACK):
+            for jb in range(2):
+                nc.tensor.transpose(accs[jb][:, P * t : P * (t + 1)], lead[:, t, P * jb : P * (jb + 1)], identity[:])
+        for jb in range(2):
+            gap[jb] = sb(f"gap{jb}", [P, S], F32)
+            nc.scalar.activation(gap[jb][:], accs[jb][:], ACT.Relu)
+        for jb in range(2):
+            block = slice(P * jb, P * (jb + 1))
+            acc = bank()
+            for t in range(PACK):
+                for n, term in enumerate((base[jb], gap[jb])):
+                    nc.tensor.matmul(acc[:, P * t : P * (t + 1)], lhsT=term[:, P * t : P * (t + 1)], rhs=identity[:],
+                                     is_transpose=True, start=n == 0, stop=n == 1)
+            rows = acc[:].rearrange("p (t j) -> p t j", t=PACK)
+            nc.scalar.copy(woven(result_bf[0][:, PACK * P * jb : PACK * P * (jb + 1)]), by_row(rows))
+            nc.scalar.copy(result[0][:, :, block], rows)
+        nc.sync.dma_start(out_rows[:, :, cols(0)], result[0][:])
+        for t in range(PACK):
+            fetch_h(1, t)
+        fetch_h(2, 0)
+        finish(1)
+        nc.scalar.copy(woven(result_bf[1][:]), by_row(result[1][:]))
+        for t in range(1, PACK):
+            fetch_h(2, t)
+        planes(0)
+        result_bf[2] = sb("result_bf2", [P, PACK * width(2)], BF16, "result_bf0")
         nc.vector.tensor_tensor(woven(result_bf[2][:]), by_row(cand[2][0][:]), by_row(cand[2][1][:]), ALU.max)
+        planes(1)
         finish(2)
         planes(2)
         for q in range(4):

@@ -4,7 +4,7 @@ import concourse.mybir as mybir
 from concourse.masks import make_identity
 
 K, T, S, N, H = 512, 2048, 512, 512, 512
-FLOPS = 4 * 2 * 512 * 512 * 512
+FLOPS = 2 * S * (3 * K * H + H * N)
 
 F32 = mybir.dt.float32
 BF16 = mybir.dt.bfloat16
@@ -18,9 +18,13 @@ ACT = mybir.ActivationFunctionType
 
 P = 128
 PACK = 4
-LIST_COLS = S // 16
+QUADRANTS = 4
+ENTRIES_A_COLUMN = 16
 WIDE = 2 * S
-CHUNKS = ((0, 256), (256, 384), (384, 512))
+BLOCKS = S // P
+HALF = S // 2
+CHUNKS = ((0, HALF), (HALF, HALF + P), (HALF + P, S))
+LAST = len(CHUNKS) - 1
 
 
 def tile_picked_triopathbnormbover_none_po_kernel(
@@ -33,336 +37,342 @@ def tile_picked_triopathbnormbover_none_po_kernel(
         ring = ctx.enter_context(tc.tile_pool(name="ring", bufs=4))
         psum = ctx.enter_context(tc.psum_pool(name="psum", bufs=8))
 
-        def sb(name, shape, dtype, tag=None):
-            return keep.tile(shape, dtype, name=name, tag=tag or name, align_bytes=64)
+        def sbuf(name, shape, dtype, after=None):
+            return keep.tile(shape, dtype, name=name, tag=after or name, align_bytes=64)
 
         def bank():
             return psum.tile([P, S], F32, name="bank")
 
-        def words_view(ap):
-            return ap[0].rearrange("p n t -> p (n t)").bitcast(I32)
+        def block(index):
+            return slice(P * index, P * (index + 1))
 
-        def load_list(name, ap):
-            tile = keep.tile([P, LIST_COLS], U16, name=name)
-            nc.sync.dma_start(tile[:], ap)
+        def as_words(packed):
+            return packed[0].rearrange("p n t -> p (n t)").bitcast(I32)
+
+        def load_list(name, source):
+            tile = keep.tile([P, S // ENTRIES_A_COLUMN], U16, name=name)
+            nc.sync.dma_start(tile[:], source)
             return tile
 
-        def load_scales(plane, first_row, cols, ap):
-            for q in range(4):
+        def load_scales(plane, first_row, source, queues=(nc.sync,)):
+            for q in range(QUADRANTS):
                 rows = slice(32 * q + first_row, 32 * q + first_row + 4)
-                nc.sync.dma_start(plane[:].bitcast(I32)[rows, cols], ap[0, 4 * q : 4 * q + 4, :].bitcast(I32))
+                queues[q % len(queues)].dma_start(plane[:].bitcast(I32)[rows, :], source[0, 4 * q : 4 * q + 4, :].bitcast(I32))
 
-        def load_words(name, ap, width):
-            tile = sb(name, [P, width], I32)
-            nc.sync.dma_start(tile[:], words_view(ap))
+        def load_words(name, source, columns):
+            tile = sbuf(name, [P, columns], I32)
+            nc.sync.dma_start(tile[:], as_words(source))
             return tile
 
-        x_plane = sb("x_plane", [P, T], U8)
+        x_plane = sbuf("x_plane", [P, T], U8)
         nc.vector.memset(x_plane[:].bitcast(I32)[:, 0 : T // 8], 0)
         nc.gpsimd.memset(x_plane[:].bitcast(I32)[:, T // 8 : T // 4], 0)
-        w_planes = [sb("w_plane_a", [P, H], U8), sb("w_plane_b", [P, H], U8)]
-        for plane in w_planes:
-            nc.vector.memset(plane[:].bitcast(I32), 0)
-        half = keep.tile([P, 1], F32, name="half")
-        nc.vector.memset(half[:], 0.5)
-        warm = keep.tile([P, 1], F32, name="warm")
-        nc.scalar.activation(warm[:], half[:], ACT.Ln, bias=half[:])
+        w31_plane_raw = sbuf("w31_plane_raw", [P, H], U8)
+        w24_plane_raw = sbuf("w24_plane_raw", [P, H], U8)
+        for plane_raw in (w31_plane_raw, w24_plane_raw):
+            nc.vector.memset(plane_raw[:].bitcast(I32), 0)
+        point_five = keep.tile([P, 1], F32, name="point_five")
+        nc.vector.memset(point_five[:], 0.5)
+        warm_up = keep.tile([P, 1], F32, name="warm_up")
+        nc.scalar.activation(warm_up[:], point_five[:], ACT.Ln, bias=point_five[:])
 
-        identity = sb("identity", [P, P], F32)
+        identity = sbuf("identity", [P, P], F32)
         make_identity(nc, identity[:])
 
-        load_scales(x_plane, 0, slice(0, T // 4), x_scales)
-        tok_three, tok_offs, tok_two = load_list("three", three), load_list("offs", offs), load_list("two", two)
-        token_lists = [tok_offs, tok_two, tok_three]
+        load_scales(x_plane, 0, x_scales, (nc.sync, nc.scalar))
+        tokens = {"b": load_list("three", three), "y": load_list("offs", offs), "d": load_list("two", two)}
         x_codes = load_words("x_codes", x_words, T)
-        all_cols = slice(0, H // 4)
-        load_scales(w_planes[0], 0, all_cols, w3_scales)
+        load_scales(w31_plane_raw, 0, w3_scales)
         w3_raw = load_words("w3_raw", w3_words, H)
-        load_scales(w_planes[0], 4, all_cols, w1_scales)
+        load_scales(w31_plane_raw, 4, w1_scales)
         w1_raw = load_words("w1_raw", w1_words, H)
-        load_scales(w_planes[1], 0, all_cols, w2_scales)
+        load_scales(w24_plane_raw, 0, w2_scales)
         w2_raw = load_words("w2_raw", w2_words, H)
-        load_scales(w_planes[1], 4, all_cols, w4_scales)
-        l1, l2, l3, l4, l6 = (load_list(name, ap) for name, ap in (("n1", n1), ("n2", n2), ("n3", n3), ("n4", n4), ("n6", n6)))
+        load_scales(w24_plane_raw, 4, w4_scales)
+        list1, list2, list3, list4, list6 = (
+            load_list(name, source) for name, source in (("n1", n1), ("n2", n2), ("n3", n3), ("n4", n4), ("n6", n6))
+        )
         gain = keep.tile([P, PACK], F32, name="gain")
         nc.sync.dma_start(gain[:], gn.rearrange("(p t) o -> p (t o)", t=PACK))
-        l5 = load_list("n5", n5)
+        list5 = load_list("n5", n5)
         w4_raw = load_words("w4_raw", w4_words, N)
-        l7, l8 = load_list("n7", n7), load_list("n8", n8)
+        list7, list8 = load_list("n7", n7), load_list("n8", n8)
+
+        def deal(name, raw, dtype, run):
+            dealt = sbuf(name, [P, H], dtype)
+            nc.vector.tensor_copy(
+                dealt[:].rearrange("p (t b i) -> p b t i", t=PACK, i=run),
+                raw[:].rearrange("p (b i t) -> p b t i", t=PACK, i=run),
+            )
+            return dealt
 
         def deal_words(name, raw):
-            dealt = sb(name, [P, H], I32)
-            nc.vector.tensor_copy(
-                dealt[:].rearrange("p (t b i) -> p b t i", t=PACK, i=4),
-                raw[:].rearrange("p (b i t) -> p b t i", t=PACK, i=4),
-            )
-            return dealt
+            return deal(name, raw, I32, 4)
 
-        def deal_scales(name, plane):
-            dealt = sb(name, [P, H], U8)
-            nc.vector.tensor_copy(
-                dealt[:].rearrange("p (t b i) -> p b t i", t=PACK, i=16),
-                plane[:].rearrange("p (b i t) -> p b t i", t=PACK, i=16),
-            )
-            return dealt
+        def deal_scales(name, raw):
+            return deal(name, raw, U8, 16)
 
-        def pick_scales(i):
-            picked = sb(f"picked_scales{i}", [P, S], U8)
-            nc.vector.tensor_copy(picked[:], x_plane[:].indirect(token_lists[i][:]))
-            return picked
+        picked_scales, picked_words = {}, {}
 
-        def pick_words(i, tag=None):
-            picked = sb(f"picked_words{i}", [P, S], U32, tag)
-            nc.vector.tensor_copy(picked[:], x_codes[:].bitcast(U32).indirect(token_lists[i][:]))
-            return picked
+        def pick_scales(stream):
+            picked_scales[stream] = sbuf(f"picked_scales_{stream}", [P, S], U8)
+            nc.vector.tensor_copy(picked_scales[stream][:], x_plane[:].indirect(tokens[stream][:]))
+
+        def pick_words(stream, after=None):
+            picked_words[stream] = sbuf(f"picked_words_{stream}", [P, S], U32, after)
+            nc.vector.tensor_copy(picked_words[stream][:], x_codes[:].bitcast(U32).indirect(tokens[stream][:]))
 
         def product(out, w_dealt, w_plane, first_row, t, codes, scales):
-            cols = slice(P * t, P * (t + 1))
             nc.tensor.matmul_mx(
-                out=out, lhsT=w_dealt[:, cols].bitcast(FP8X4), lhsT_scale=w_plane[first_row:P, cols],
-                rhs=codes.bitcast(FP8X4), rhs_scale=scales, start=True, stop=True,
+                out=out, lhsT=w_dealt[:, block(t)].bitcast(FP8X4), lhsT_scale=w_plane[first_row:P, block(t)],
+                rhs=codes[:].bitcast(FP8X4), rhs_scale=scales[:], start=True, stop=True,
             )
 
-        tok_scales, tok_words = {}, {}
+        def add_transposed(out, left, right):
+            nc.tensor.matmul(out, lhsT=left, rhs=identity[:], is_transpose=True, start=True, stop=False)
+            nc.tensor.matmul(out, lhsT=right, rhs=identity[:], is_transpose=True, start=False, stop=True)
+
         y_win, d_win, b_abs, b_log, b_far = {}, {}, {}, {}, {}
+        y_fetched, sums, m1, m1_gained, m1_gained_neg = {}, {}, {}, {}, {}
 
         def project_y(t):
             acc = bank()
-            product(acc[:], w1_dealt, plane_a, 4, t, tok_words[0][:], tok_scales[0][:])
-            y_win[t] = sb(f"y_win{t}", [P, WIDE], F32)
+            product(acc[:], w1_dealt, w31_plane, 4, t, picked_words["y"], picked_scales["y"])
+            y_win[t] = sbuf(f"y_win{t}", [P, WIDE], F32)
             nc.scalar.copy(y_win[t][:, 0:S], acc[:])
 
         def project_d(t):
             acc = bank()
-            product(acc[:], w2_dealt, plane_b, 0, t, tok_words[1][:], tok_scales[1][:])
-            d_win[t] = sb(f"d_win{t}", [P, WIDE], F32)
+            product(acc[:], w2_dealt, w24_plane, 0, t, picked_words["d"], picked_scales["d"])
+            d_win[t] = sbuf(f"d_win{t}", [P, WIDE], F32)
             nc.scalar.copy(d_win[t][:, 0:S], acc[:])
 
         def project_b(t):
             acc = bank()
-            product(acc[:], w3_dealt, plane_a, 0, t, tok_words[2][:], tok_scales[2][:])
-            b_abs[t] = sb(f"b_abs{t}", [P, S], F32)
+            product(acc[:], w3_dealt, w31_plane, 0, t, picked_words["b"], picked_scales["b"])
+            b_abs[t] = sbuf(f"b_abs{t}", [P, S], F32)
             nc.scalar.activation(b_abs[t][:], acc[:], ACT.Abs)
 
         def log_b(t):
-            b_log[t] = sb(f"b_log{t}", [P, WIDE], F32)
-            nc.scalar.activation(b_log[t][:, 0:S], b_abs[t][:], ACT.Ln, bias=half[:])
+            b_log[t] = sbuf(f"b_log{t}", [P, WIDE], F32)
+            nc.scalar.activation(b_log[t][:, 0:S], b_abs[t][:], ACT.Ln, bias=point_five[:])
 
         def fetch_b(t):
-            b_far[t] = sb(f"b_far{t}", [P, S], F32)
-            nc.scalar.activation(b_far[t][:], b_log[t][:].indirect(l6[:]), ACT.Exp)
+            b_far[t] = sbuf(f"b_far{t}", [P, S], F32)
+            nc.scalar.activation(b_far[t][:], b_log[t][:].indirect(list6[:]), ACT.Exp)
 
-        logs, recips, factor = {}, {}, {}
+        def fetch_y(t, side):
+            y_fetched[t, side] = ring.tile([P, S], F32, name="y_fetched", bufs=2)
+            nc.vector.tensor_copy(y_fetched[t, side][:], y_win[t][:].indirect((list1, list2)[side][:]))
+
+        def add_d(t, side):
+            sums[t, side] = ring.tile([P, S], F32, name="sums")
+            nc.vector.tensor_tensor(
+                sums[t, side][:], d_win[t][:].indirect((list3, list4)[side][:]), y_fetched[t, side][:], ALU.add
+            )
+
+        def larger(t):
+            m1[t] = sbuf(f"m1_{t}", [P, S], F32)
+            nc.vector.tensor_tensor(m1[t][:], sums[t, 0][:], sums[t, 1][:], ALU.max)
+
+        def apply_gain(t):
+            m1_gained_neg[t] = sbuf(f"m1_gained_neg{t}", [P, WIDE], F32, f"y_win{t}")
+            nc.scalar.activation(m1_gained_neg[t][:, 0:S], m1[t][:], ACT.Copy, scale=gain_neg[:, t : t + 1])
+            m1_gained[t] = sbuf(f"m1_gained{t}", [P, S], F32)
+            nc.scalar.activation(m1_gained[t][:], m1[t][:], ACT.Copy, scale=gain[:, t : t + 1])
+
+        log_turned, reciprocal_turned, reciprocal_bank = {}, {}, {}
 
         def log_denominator(jb):
             acc = bank()
             for t in range(PACK):
-                for term, first in ((b_far[t], True), (b_abs[t], False)):
-                    nc.tensor.matmul(acc[:, P * t : P * (t + 1)], lhsT=term[:, P * jb : P * (jb + 1)], rhs=identity[:],
-                                     is_transpose=True, start=first, stop=not first)
-            logs[jb] = sb(f"logs{jb}", [P, S], F32)
-            nc.scalar.activation(logs[jb][:], acc[:], ACT.Ln)
+                add_transposed(acc[:, block(t)], b_far[t][:, block(jb)], b_abs[t][:, block(jb)])
+            log_turned[jb] = sbuf(f"log_turned{jb}", [P, S], F32)
+            nc.scalar.activation(log_turned[jb][:], acc[:], ACT.Ln)
 
         def reciprocal(jb):
-            recips[jb] = sb(f"recips{jb}", [P, S], F32)
-            nc.scalar.activation(recips[jb][:], logs[jb][:], ACT.Exp, scale=-1.0)
-            factor[jb] = bank()
+            reciprocal_turned[jb] = sbuf(f"reciprocal_turned{jb}", [P, S], F32)
+            nc.scalar.activation(reciprocal_turned[jb][:], log_turned[jb][:], ACT.Exp, scale=-1.0)
+            reciprocal_bank[jb] = bank()
             for t in range(PACK):
-                nc.tensor.transpose(factor[jb][:, P * t : P * (t + 1)], recips[jb][:, P * t : P * (t + 1)], identity[:])
+                nc.tensor.transpose(reciprocal_bank[jb][:, block(t)], reciprocal_turned[jb][:, block(t)], identity[:])
 
-        fetched, sums, m1, m1_neg = {}, {}, {}, {}
-
-        def fetch_y(t, u):
-            fetched[t, u] = ring.tile([P, S], F32, name="fetched")
-            nc.vector.tensor_copy(fetched[t, u][:], y_win[t][:].indirect((l1, l2)[u][:]))
-
-        def add_d(t, u):
-            sums[t, u] = ring.tile([P, S], F32, name="sums")
-            nc.vector.tensor_tensor(sums[t, u][:], d_win[t][:].indirect((l3, l4)[u][:]), fetched[t, u][:], ALU.add)
-
-        m1_raw = {}
-
-        def larger(t):
-            m1_raw[t] = sb(f"m1_raw{t}", [P, S], F32)
-            nc.vector.tensor_tensor(m1_raw[t][:], sums[t, 0][:], sums[t, 1][:], ALU.max)
-
-        def gained(t):
-            raw = m1_raw[t]
-            m1_neg[t] = sb(f"m1_neg{t}", [P, S], F32)
-            nc.scalar.activation(m1_neg[t][:], raw[:], ACT.Copy, scale=gain_neg[:, t : t + 1])
-            m1[t] = sb(f"m1_{t}", [P, S], F32)
-            nc.scalar.activation(m1[t][:], raw[:], ACT.Copy, scale=gain[:, t : t + 1])
-
-        for i in (2, 0, 1):
-            tok_scales[i] = pick_scales(i)
-        tok_words[2] = pick_words(2)
+        for stream in ("b", "y", "d"):
+            pick_scales(stream)
+        pick_words("b")
         w3_dealt = deal_words("w3_dealt", w3_raw)
-        plane_a = deal_scales("plane_a", w_planes[0])
+        w31_plane = deal_scales("w31_plane", w31_plane_raw)
         for t in range(PACK):
             project_b(t)
-        tok_words[0] = pick_words(0, "w_plane_a")
+        pick_words("y", "w31_plane_raw")
         w1_dealt = deal_words("w1_dealt", w1_raw)
-        tok_words[1] = pick_words(1, "w1_raw")
+        pick_words("d", "w1_raw")
         w2_dealt = deal_words("w2_dealt", w2_raw)
-        plane_b = deal_scales("plane_b", w_planes[1])
+        w24_plane = deal_scales("w24_plane", w24_plane_raw)
+
         project_y(0)
         project_y(1)
         project_d(0)
         for t in range(PACK):
             log_b(t)
-        project_d(1)
         project_y(2)
+        project_d(1)
+        project_y(3)
         project_d(2)
         for t in range(PACK):
             fetch_b(t)
-        project_y(3)
         project_d(3)
         gain_neg = keep.tile([P, PACK], F32, name="gain_neg")
         nc.scalar.activation(gain_neg[:], gain[:], ACT.Copy, scale=-1.0)
-        fetch_y(0, 0)
-        fetch_y(0, 1)
-        add_d(0, 0)
-        add_d(0, 1)
-        for t in range(1, PACK):
+
+        for t in range(PACK):
             fetch_y(t, 0)
-            larger(t - 1)
+            if t > 0:
+                larger(t - 1)
             fetch_y(t, 1)
             add_d(t, 0)
             add_d(t, 1)
         w4_dealt = deal_words("w4_dealt", w4_raw)
         larger(PACK - 1)
-        gained(0)
-        for jb in range(PACK):
+
+        apply_gain(0)
+        for jb in range(BLOCKS):
             log_denominator(jb)
-        gained(1)
+        apply_gain(1)
         reciprocal(0)
         reciprocal(1)
-        gained(2)
-        gained(3)
+        apply_gain(2)
+        apply_gain(3)
         reciprocal(2)
         reciprocal(3)
 
-        def list_cols(c):
-            return slice(CHUNKS[c][0] // 16, CHUNKS[c][1] // 16)
+        def by_row(tiles):
+            return tiles.rearrange("p t (c i) -> p c t i", i=2)
+
+        def woven(tile):
+            return tile.rearrange("p (c i t) -> p c t i", i=2, t=PACK)
+
+        def bank_rows(acc):
+            return acc[:].rearrange("p (t j) -> p t j", t=PACK)
+
+        numerator = sbuf("numerator", [P, PACK, S], F32)
+        z_bf = [sbuf(f"z_bf{jb}", [P, PACK * P], BF16) for jb in range(BLOCKS)]
+        z_codes = [sbuf(f"z_codes{jb}", [P, P], U32) for jb in range(BLOCKS)]
+        z_plane = [sbuf(f"z_plane{jb}", [P, P], U8) for jb in range(BLOCKS)]
+        h_win = [sbuf(f"h_win{t}", [P, S], F32) for t in range(PACK)]
+        h_less = [sbuf(f"h_less{side}", [P, PACK, HALF], F32) for side in range(2)]
+        h_less_chunk = [h_less[0][:], h_less[1][:, :, block(0)], h_less[1][:, :, block(1)]]
+
+        def make_z(jb):
+            nc.vector.tensor_tensor(
+                woven(z_bf[jb][:]), by_row(numerator[:, :, block(jb)]), by_row(bank_rows(reciprocal_bank[jb])), ALU.mult
+            )
+
+        def quantise_z(jb):
+            nc.vector.quantize_mx(out=z_codes[jb][:].bitcast(FP8X4), scales=z_plane[jb][:], in_=z_bf[jb][:])
+
+        for t in range(PACK):
+            nc.vector.tensor_tensor(numerator[:, t, :], m1_gained_neg[t][:].indirect(list5[:]), m1_gained[t][:], ALU.add)
+        make_z(0)
+        for jb in range(1, BLOCKS):
+            make_z(jb)
+            quantise_z(jb - 1)
+        quantise_z(BLOCKS - 1)
+
+        h_bank = {}
+        for t in range(PACK):
+            for side in range(2):
+                h_bank[side, t] = bank()
+                for part in range(2):
+                    jb = 2 * side + part
+                    product(h_bank[side, t][:, block(part)], w4_dealt, w24_plane, 4, t, z_codes[jb], z_plane[jb])
+                nc.scalar.copy(h_win[t][:, HALF * side : HALF * (side + 1)], h_bank[side, t][:, 0:HALF])
+        for side in range(2):
+            for t in range(PACK):
+                nc.scalar.activation(h_less[side][:, t, :], h_bank[side, t][:, 0:HALF], ACT.Copy, scale=-0.75)
+
+        def columns(c):
+            return slice(*CHUNKS[c])
+
+        def entries(c):
+            return slice(CHUNKS[c][0] // ENTRIES_A_COLUMN, CHUNKS[c][1] // ENTRIES_A_COLUMN)
 
         def width(c):
             return CHUNKS[c][1] - CHUNKS[c][0]
 
-        def cols(c):
-            return slice(*CHUNKS[c])
-
-        def by_row(ap):
-            return ap.rearrange("p t (c i) -> p c t i", i=2)
-
-        def woven(ap):
-            return ap.rearrange("p (c i t) -> p c t i", i=2, t=PACK)
-
-        diff = [sb(f"diff{c}", [P, PACK, width(c)], F32) for c in range(3)]
-        z_bf = [sb(f"z_bf{c}", [P, PACK * width(c)], BF16) for c in range(3)]
-        z_codes = [sb(f"z_codes{c}", [P, width(c)], U32) for c in range(3)]
-        z_scales = [sb(f"z_scales{c}", [P, width(c)], U8) for c in range(3)]
-        h_win = [sb(f"h_win{t}", [P, S], F32) for t in range(PACK)]
-        h_part = [sb(f"h_part{c}", [P, PACK, width(c)], F32) for c in range(3)]
-
-        def fetch_m1(c, t):
-            nc.vector.tensor_tensor(diff[c][:, t, :], m1_neg[t][:].indirect(l5[:, list_cols(c)]), m1[t][:, cols(c)], ALU.add)
-
-        def make_z(c):
-            for first in range(0, width(c), P):
-                jb = (CHUNKS[c][0] + first) // P
-                nc.vector.tensor_tensor(
-                    woven(z_bf[c][:, PACK * first : PACK * (first + P)]), by_row(diff[c][:, :, first : first + P]),
-                    by_row(factor[jb][:].rearrange("p (t j) -> p t j", t=PACK)), ALU.mult,
-                )
-
-        def last_product(c):
-            nc.vector.quantize_mx(out=z_codes[c][:].bitcast(FP8X4), scales=z_scales[c][:], in_=z_bf[c][:])
-            accs = []
-            for t in range(PACK):
-                acc = bank()
-                product(acc[:, 0 : width(c)], w4_dealt, plane_b, 4, t, z_codes[c][:], z_scales[c][:])
-                nc.scalar.copy(h_win[t][:, cols(c)], acc[:, 0 : width(c)])
-                accs.append(acc)
-            for t in range(PACK):
-                nc.scalar.activation(h_part[c][:, t, :], accs[t][:, 0 : width(c)], ACT.Copy, scale=-0.75)
-
-        for t in range(PACK):
-            fetch_m1(0, t)
-        for c in (1, 2):
-            fetch_m1(c, 0)
-            make_z(c - 1)
-            fetch_m1(c, 1)
-            last_product(c - 1)
-            fetch_m1(c, 2)
-            fetch_m1(c, 3)
-        make_z(2)
-        last_product(2)
-
-        cand = [[sb(f"cand{c}_{u}", [P, PACK, width(c)], F32) for u in range(2)] for c in range(3)]
-        result = [sb(f"result{c}", [P, PACK, width(c)], F32) for c in range(3)]
-        result_bf = {c: sb(f"result_bf{c}", [P, PACK * width(c)], BF16) for c in range(2)}
-        out_codes = sb("out_codes", [P, S], U32)
-        out_plane = sb("out_plane", [P, S], U8)
+        h_fetched = [[sbuf(f"h_fetched{c}_{side}", [P, PACK, width(c)], F32) for side in range(2)] for c in range(len(CHUNKS))]
+        result = [sbuf(f"result{c}", [P, PACK, width(c)], F32) for c in range(len(CHUNKS))]
+        result_bf = {0: sbuf("result_bf0", [P, PACK * width(0)], BF16)}
+        out_codes = sbuf("out_codes", [P, S], U32)
+        out_plane = sbuf("out_plane", [P, S], U8)
         out_rows = out_0.rearrange("(p t) j -> p t j", t=PACK)
 
         def fetch_h(c, t):
-            for u, lst in enumerate((l7, l8)):
-                nc.vector.tensor_tensor(cand[c][u][:, t, :], h_win[t][:].indirect(lst[:, list_cols(c)]), h_part[c][:, t, :], ALU.add)
+            for side, places in enumerate((list7, list8)):
+                nc.vector.tensor_tensor(
+                    h_fetched[c][side][:, t, :], h_win[t][:].indirect(places[:, entries(c)]), h_less_chunk[c][:, t, :], ALU.add
+                )
 
         def finish(c):
-            nc.vector.tensor_tensor(result[c][:], cand[c][0][:], cand[c][1][:], ALU.max)
-            nc.sync.dma_start(out_rows[:, :, cols(c)], result[c][:])
+            nc.vector.tensor_tensor(result[c][:], h_fetched[c][0][:], h_fetched[c][1][:], ALU.max)
+            nc.sync.dma_start(out_rows[:, :, columns(c)], result[c][:])
 
-        def planes(c):
-            nc.vector.quantize_mx(out=out_codes[:, cols(c)].bitcast(FP8X4), scales=out_plane[:, cols(c)], in_=result_bf[c][:])
-            nc.sync.dma_start(words_view(out_1)[:, cols(c)], out_codes[:, cols(c)].bitcast(I32))
+        def quantise_result(c):
+            nc.vector.quantize_mx(
+                out=out_codes[:, columns(c)].bitcast(FP8X4), scales=out_plane[:, columns(c)], in_=result_bf[c][:]
+            )
 
-        first, lead = cand[0]
+        def store_codes(queue, span):
+            queue.dma_start(as_words(out_1)[:, span], out_codes[:, span].bitcast(I32))
+
+        u, lead = h_fetched[0]
+        chunk_blocks = range(width(0) // P)
         for t in range(PACK):
-            nc.vector.tensor_copy(first[:, t, :], h_win[t][:].indirect(l7[:, list_cols(0)]))
+            nc.vector.tensor_copy(u[:, t, :], h_win[t][:].indirect(list7[:, entries(0)]))
         for t in range(PACK):
-            nc.vector.tensor_tensor(lead[:, t, :], h_win[t][:].indirect(l8[:, list_cols(0)]), first[:, t, :], ALU.subtract)
+            nc.vector.tensor_tensor(lead[:, t, :], h_win[t][:].indirect(list8[:, entries(0)]), u[:, t, :], ALU.subtract)
         base, gap = {}, {}
-        for jb in range(2):
-            block = slice(P * jb, P * (jb + 1))
+        for jb in chunk_blocks:
             acc = bank()
             for t in range(PACK):
-                for n, term in enumerate((h_part[0], first)):
-                    nc.tensor.matmul(acc[:, P * t : P * (t + 1)], lhsT=term[:, t, block], rhs=identity[:],
-                                     is_transpose=True, start=n == 0, stop=n == 1)
-            base[jb] = sb(f"base{jb}", [P, S], F32)
+                add_transposed(acc[:, block(t)], h_less_chunk[0][:, t, block(jb)], u[:, t, block(jb)])
+            base[jb] = sbuf(f"base{jb}", [P, S], F32)
             nc.scalar.copy(base[jb][:], acc[:])
-        accs = [bank(), bank()]
+        lead_bank = [bank() for jb in chunk_blocks]
         for t in range(PACK):
-            for jb in range(2):
-                nc.tensor.transpose(accs[jb][:, P * t : P * (t + 1)], lead[:, t, P * jb : P * (jb + 1)], identity[:])
-        for jb in range(2):
-            gap[jb] = sb(f"gap{jb}", [P, S], F32)
-            nc.scalar.activation(gap[jb][:], accs[jb][:], ACT.Relu)
-        for jb in range(2):
-            block = slice(P * jb, P * (jb + 1))
+            for jb in chunk_blocks:
+                nc.tensor.transpose(lead_bank[jb][:, block(t)], lead[:, t, block(jb)], identity[:])
+        for jb in chunk_blocks:
+            gap[jb] = sbuf(f"gap{jb}", [P, S], F32)
+            nc.scalar.activation(gap[jb][:], lead_bank[jb][:], ACT.Relu)
+        for jb in chunk_blocks:
             acc = bank()
             for t in range(PACK):
-                for n, term in enumerate((base[jb], gap[jb])):
-                    nc.tensor.matmul(acc[:, P * t : P * (t + 1)], lhsT=term[:, P * t : P * (t + 1)], rhs=identity[:],
-                                     is_transpose=True, start=n == 0, stop=n == 1)
-            rows = acc[:].rearrange("p (t j) -> p t j", t=PACK)
-            nc.scalar.copy(woven(result_bf[0][:, PACK * P * jb : PACK * P * (jb + 1)]), by_row(rows))
-            nc.scalar.copy(result[0][:, :, block], rows)
-        nc.sync.dma_start(out_rows[:, :, cols(0)], result[0][:])
+                add_transposed(acc[:, block(t)], base[jb][:, block(t)], gap[jb][:, block(t)])
+            nc.scalar.copy(woven(result_bf[0][:, PACK * P * jb : PACK * P * (jb + 1)]), by_row(bank_rows(acc)))
+            nc.scalar.copy(result[0][:, :, block(jb)], bank_rows(acc))
+        nc.sync.dma_start(out_rows[:, :, columns(0)], result[0][:])
+
         for t in range(PACK):
             fetch_h(1, t)
-        fetch_h(2, 0)
+        fetch_h(LAST, 0)
         finish(1)
+        result_bf[1] = sbuf("result_bf1", [P, PACK * width(1)], BF16, f"gap{chunk_blocks[-1]}")
         nc.scalar.copy(woven(result_bf[1][:]), by_row(result[1][:]))
+
         for t in range(1, PACK):
-            fetch_h(2, t)
-        planes(0)
-        result_bf[2] = sb("result_bf2", [P, PACK * width(2)], BF16, "result_bf0")
-        nc.vector.tensor_tensor(woven(result_bf[2][:]), by_row(cand[2][0][:]), by_row(cand[2][1][:]), ALU.max)
-        planes(1)
-        finish(2)
-        planes(2)
-        for q in range(4):
-            queue = nc.scalar if q % 2 else nc.sync
+            fetch_h(LAST, t)
+        quantise_result(0)
+        store_codes(nc.sync, columns(0))
+        result_bf[LAST] = sbuf(f"result_bf{LAST}", [P, PACK * width(LAST)], BF16, "result_bf0")
+        nc.vector.tensor_tensor(
+            woven(result_bf[LAST][:]), by_row(h_fetched[LAST][0][:]), by_row(h_fetched[LAST][1][:]), ALU.max
+        )
+        quantise_result(1)
+        finish(LAST)
+        quantise_result(LAST)
+
+        store_codes(nc.scalar, slice(HALF, S))
+        for q in range(QUADRANTS):
+            queue = nc.scalar if q == QUADRANTS - 1 else nc.sync
             queue.dma_start(out_2[0, 4 * q : 4 * q + 4, :].bitcast(I32), out_plane[:].bitcast(I32)[32 * q : 32 * q + 4, :])

from contextlib import ExitStack

import concourse.mybir as mybir
from concourse.masks import make_identity

K, T, S, N, H = 512, 2048, 512, 512, 512
FLOPS = 2 * S * (3 * K * H + H * N)

F32 = mybir.dt.float32
BF16 = mybir.dt.bfloat16
I32 = mybir.dt.int32
U32 = mybir.dt.uint32
U16 = mybir.dt.uint16
U8 = mybir.dt.uint8
FP8X4 = mybir.dt.float8_e4m3fn_x4
ALU = mybir.AluOpType
ACT = mybir.ActivationFunctionType

P = 128
PACK = 4
QUADRANTS = 4
ENTRIES_A_COLUMN = 16
WIDE = 2 * S
BLOCKS = S // P
HALF = S // 2
CHUNKS = ((0, HALF), (HALF, HALF + P), (HALF + P, S))
LAST = len(CHUNKS) - 1


def tile_picked_triopathbnormbover_none_po_kernel(
    tc, x_words, x_scales, w1_words, w1_scales, w2_words, w2_scales, w3_words, w3_scales, gn,
    w4_words, w4_scales, offs, two, three, n1, n2, n3, n4, n5, n6, n7, n8, out_0, out_1, out_2,
):
    nc = tc.nc
    with ExitStack() as ctx:
        keep = ctx.enter_context(tc.tile_pool(name="keep", bufs=1))
        ring = ctx.enter_context(tc.tile_pool(name="ring", bufs=4))
        psum = ctx.enter_context(tc.psum_pool(name="psum", bufs=8))

        def sbuf(name, shape, dtype, after=None):
            return keep.tile(shape, dtype, name=name, tag=after or name, align_bytes=64)

        def bank():
            return psum.tile([P, S], F32, name="bank")

        def block(index):
            return slice(P * index, P * (index + 1))

        def as_words(packed):
            return packed[0].rearrange("p n t -> p (n t)").bitcast(I32)

        def load_list(name, source):
            tile = keep.tile([P, S // ENTRIES_A_COLUMN], U16, name=name)
            nc.sync.dma_start(tile[:], source)
            return tile

        def load_scales(plane, first_row, source, queues=(nc.sync,)):
            for q in range(QUADRANTS):
                rows = slice(32 * q + first_row, 32 * q + first_row + 4)
                queues[q % len(queues)].dma_start(plane[:].bitcast(I32)[rows, :], source[0, 4 * q : 4 * q + 4, :].bitcast(I32))

        def load_words(name, source, columns):
            tile = sbuf(name, [P, columns], I32)
            nc.sync.dma_start(tile[:], as_words(source))
            return tile

        x_plane = sbuf("x_plane", [P, T], U8)
        nc.vector.memset(x_plane[:].bitcast(I32)[:, 0 : T // 8], 0)
        nc.gpsimd.memset(x_plane[:].bitcast(I32)[:, T // 8 : T // 4], 0)
        w31_plane_raw = sbuf("w31_plane_raw", [P, H], U8)
        w24_plane_raw = sbuf("w24_plane_raw", [P, H], U8)
        for plane_raw in (w31_plane_raw, w24_plane_raw):
            nc.vector.memset(plane_raw[:].bitcast(I32), 0)
        point_five = keep.tile([P, 1], F32, name="point_five")
        nc.vector.memset(point_five[:], 0.5)
        warm_up = keep.tile([P, 1], F32, name="warm_up")
        nc.scalar.activation(warm_up[:], point_five[:], ACT.Ln, bias=point_five[:])

        identity = sbuf("identity", [P, P], F32)
        make_identity(nc, identity[:])

        load_scales(x_plane, 0, x_scales, (nc.sync, nc.scalar))
        tokens = {"b": load_list("three", three), "y": load_list("offs", offs), "d": load_list("two", two)}
        x_codes = load_words("x_codes", x_words, T)
        load_scales(w31_plane_raw, 0, w3_scales)
        w3_raw = load_words("w3_raw", w3_words, H)
        load_scales(w31_plane_raw, 4, w1_scales)
        w1_raw = load_words("w1_raw", w1_words, H)
        load_scales(w24_plane_raw, 0, w2_scales)
        w2_raw = load_words("w2_raw", w2_words, H)
        load_scales(w24_plane_raw, 4, w4_scales)
        list1, list2, list3, list4, list6 = (
            load_list(name, source) for name, source in (("n1", n1), ("n2", n2), ("n3", n3), ("n4", n4), ("n6", n6))
        )
        gain = keep.tile([P, PACK], F32, name="gain")
        nc.sync.dma_start(gain[:], gn.rearrange("(p t) o -> p (t o)", t=PACK))
        list5 = load_list("n5", n5)
        w4_raw = load_words("w4_raw", w4_words, N)
        list7, list8 = load_list("n7", n7), load_list("n8", n8)

        def deal(name, raw, dtype, run):
            dealt = sbuf(name, [P, H], dtype)
            nc.vector.tensor_copy(
                dealt[:].rearrange("p (t b i) -> p b t i", t=PACK, i=run),
                raw[:].rearrange("p (b i t) -> p b t i", t=PACK, i=run),
            )
            return dealt

        def deal_words(name, raw):
            return deal(name, raw, I32, 4)

        def deal_scales(name, raw):
            return deal(name, raw, U8, 16)

        picked_scales, picked_words = {}, {}

        def pick_scales(stream):
            picked_scales[stream] = sbuf(f"picked_scales_{stream}", [P, S], U8)
            nc.vector.tensor_copy(picked_scales[stream][:], x_plane[:].indirect(tokens[stream][:]))

        def pick_words(stream, after=None):
            picked_words[stream] = sbuf(f"picked_words_{stream}", [P, S], U32, after)
            nc.vector.tensor_copy(picked_words[stream][:], x_codes[:].bitcast(U32).indirect(tokens[stream][:]))

        def product(out, w_dealt, w_plane, first_row, t, codes, scales):
            nc.tensor.matmul_mx(
                out=out, lhsT=w_dealt[:, block(t)].bitcast(FP8X4), lhsT_scale=w_plane[first_row:P, block(t)],
                rhs=codes[:].bitcast(FP8X4), rhs_scale=scales[:], start=True, stop=True,
            )

        def add_transposed(out, left, right):
            nc.tensor.matmul(out, lhsT=left, rhs=identity[:], is_transpose=True, start=True, stop=False)
            nc.tensor.matmul(out, lhsT=right, rhs=identity[:], is_transpose=True, start=False, stop=True)

        y_win, d_win, b_abs, b_log, b_far = {}, {}, {}, {}, {}
        y_fetched, sums, m1, m1_gained, m1_gained_neg = {}, {}, {}, {}, {}

        def project_y(t):
            acc = bank()
            product(acc[:], w1_dealt, w31_plane, 4, t, picked_words["y"], picked_scales["y"])
            y_win[t] = sbuf(f"y_win{t}", [P, WIDE], F32)
            nc.scalar.copy(y_win[t][:, 0:S], acc[:])

        def project_d(t):
            acc = bank()
            product(acc[:], w2_dealt, w24_plane, 0, t, picked_words["d"], picked_scales["d"])
            d_win[t] = sbuf(f"d_win{t}", [P, WIDE], F32)
            nc.scalar.copy(d_win[t][:, 0:S], acc[:])

        def project_b(t):
            acc = bank()
            product(acc[:], w3_dealt, w31_plane, 0, t, picked_words["b"], picked_scales["b"])
            b_abs[t] = sbuf(f"b_abs{t}", [P, S], F32)
            nc.scalar.activation(b_abs[t][:], acc[:], ACT.Abs)

        def log_b(t):
            b_log[t] = sbuf(f"b_log{t}", [P, WIDE], F32)
            nc.scalar.activation(b_log[t][:, 0:S], b_abs[t][:], ACT.Ln, bias=point_five[:])

        def fetch_b(t):
            b_far[t] = sbuf(f"b_far{t}", [P, S], F32)
            nc.scalar.activation(b_far[t][:], b_log[t][:].indirect(list6[:]), ACT.Exp)

        def fetch_y(t, side):
            y_fetched[t, side] = ring.tile([P, S], F32, name="y_fetched", bufs=2)
            nc.vector.tensor_copy(y_fetched[t, side][:], y_win[t][:].indirect((list1, list2)[side][:]))

        def add_d(t, side):
            sums[t, side] = ring.tile([P, S], F32, name="sums")
            nc.vector.tensor_tensor(
                sums[t, side][:], d_win[t][:].indirect((list3, list4)[side][:]), y_fetched[t, side][:], ALU.add
            )

        def larger(t):
            m1[t] = sbuf(f"m1_{t}", [P, S], F32)
            nc.vector.tensor_tensor(m1[t][:], sums[t, 0][:], sums[t, 1][:], ALU.max)

        def apply_gain(t):
            m1_gained_neg[t] = sbuf(f"m1_gained_neg{t}", [P, WIDE], F32, f"y_win{t}")
            nc.scalar.activation(m1_gained_neg[t][:, 0:S], m1[t][:], ACT.Copy, scale=gain_neg[:, t : t + 1])
            m1_gained[t] = sbuf(f"m1_gained{t}", [P, S], F32)
            nc.scalar.activation(m1_gained[t][:], m1[t][:], ACT.Copy, scale=gain[:, t : t + 1])

        log_turned, reciprocal_turned, reciprocal_bank = {}, {}, {}

        def log_denominator(jb):
            acc = bank()
            for t in range(PACK):
                add_transposed(acc[:, block(t)], b_far[t][:, block(jb)], b_abs[t][:, block(jb)])
            log_turned[jb] = sbuf(f"log_turned{jb}", [P, S], F32)
            nc.scalar.activation(log_turned[jb][:], acc[:], ACT.Ln)

        def reciprocal(jb):
            reciprocal_turned[jb] = sbuf(f"reciprocal_turned{jb}", [P, S], F32)
            nc.scalar.activation(reciprocal_turned[jb][:], log_turned[jb][:], ACT.Exp, scale=-1.0)
            reciprocal_bank[jb] = bank()
            for t in range(PACK):
                nc.tensor.transpose(reciprocal_bank[jb][:, block(t)], reciprocal_turned[jb][:, block(t)], identity[:])

        for stream in ("b", "y", "d"):
            pick_scales(stream)
        pick_words("b")
        w3_dealt = deal_words("w3_dealt", w3_raw)
        w31_plane = deal_scales("w31_plane", w31_plane_raw)
        for t in range(PACK):
            project_b(t)
        pick_words("y", "w31_plane_raw")
        w1_dealt = deal_words("w1_dealt", w1_raw)
        pick_words("d", "w1_raw")
        w2_dealt = deal_words("w2_dealt", w2_raw)
        w24_plane = deal_scales("w24_plane", w24_plane_raw)

        project_y(0)
        project_y(1)
        project_d(0)
        for t in range(PACK):
            log_b(t)
        project_y(2)
        project_d(1)
        project_y(3)
        project_d(2)
        for t in range(PACK):
            fetch_b(t)
        project_d(3)
        gain_neg = keep.tile([P, PACK], F32, name="gain_neg")
        nc.scalar.activation(gain_neg[:], gain[:], ACT.Copy, scale=-1.0)

        for t in range(PACK):
            fetch_y(t, 0)
            if t > 0:
                larger(t - 1)
            fetch_y(t, 1)
            add_d(t, 0)
            add_d(t, 1)
        w4_dealt = deal_words("w4_dealt", w4_raw)
        larger(PACK - 1)

        apply_gain(0)
        for jb in range(BLOCKS):
            log_denominator(jb)
        apply_gain(1)
        reciprocal(0)
        reciprocal(1)
        apply_gain(2)
        apply_gain(3)
        reciprocal(2)
        reciprocal(3)

        def by_row(tiles):
            return tiles.rearrange("p t (c i) -> p c t i", i=2)

        def woven(tile):
            return tile.rearrange("p (c i t) -> p c t i", i=2, t=PACK)

        def bank_rows(acc):
            return acc[:].rearrange("p (t j) -> p t j", t=PACK)

        numerator = sbuf("numerator", [P, PACK, S], F32)
        z_bf = [sbuf(f"z_bf{jb}", [P, PACK * P], BF16) for jb in range(BLOCKS)]
        z_codes = [sbuf(f"z_codes{jb}", [P, P], U32) for jb in range(BLOCKS)]
        z_plane = [sbuf(f"z_plane{jb}", [P, P], U8) for jb in range(BLOCKS)]
        h_win = [sbuf(f"h_win{t}", [P, S], F32) for t in range(PACK)]
        h_less = [sbuf(f"h_less{side}", [P, PACK, HALF], F32) for side in range(2)]
        h_less_chunk = [h_less[0][:], h_less[1][:, :, block(0)], h_less[1][:, :, block(1)]]

        def make_z(jb):
            nc.vector.tensor_tensor(
                woven(z_bf[jb][:]), by_row(numerator[:, :, block(jb)]), by_row(bank_rows(reciprocal_bank[jb])), ALU.mult
            )

        def quantise_z(jb):
            nc.vector.quantize_mx(out=z_codes[jb][:].bitcast(FP8X4), scales=z_plane[jb][:], in_=z_bf[jb][:])

        for t in range(PACK):
            nc.vector.tensor_tensor(numerator[:, t, :], m1_gained_neg[t][:].indirect(list5[:]), m1_gained[t][:], ALU.add)
        make_z(0)
        for jb in range(1, BLOCKS):
            make_z(jb)
            quantise_z(jb - 1)
        quantise_z(BLOCKS - 1)

        h_bank = {}
        for t in range(PACK):
            for side in range(2):
                h_bank[side, t] = bank()
                for part in range(2):
                    jb = 2 * side + part
                    product(h_bank[side, t][:, block(part)], w4_dealt, w24_plane, 4, t, z_codes[jb], z_plane[jb])
                nc.scalar.copy(h_win[t][:, HALF * side : HALF * (side + 1)], h_bank[side, t][:, 0:HALF])
        for side in range(2):
            for t in range(PACK):
                nc.scalar.activation(h_less[side][:, t, :], h_bank[side, t][:, 0:HALF], ACT.Copy, scale=-0.75)

        def columns(c):
            return slice(*CHUNKS[c])

        def entries(c):
            return slice(CHUNKS[c][0] // ENTRIES_A_COLUMN, CHUNKS[c][1] // ENTRIES_A_COLUMN)

        def width(c):
            return CHUNKS[c][1] - CHUNKS[c][0]

        h_fetched = [[sbuf(f"h_fetched{c}_{side}", [P, PACK, width(c)], F32) for side in range(2)] for c in range(len(CHUNKS))]
        result = [sbuf(f"result{c}", [P, PACK, width(c)], F32) for c in range(len(CHUNKS))]
        result_bf = {0: sbuf("result_bf0", [P, PACK * width(0)], BF16)}
        out_codes = sbuf("out_codes", [P, S], U32)
        out_plane = sbuf("out_plane", [P, S], U8)
        out_rows = out_0.rearrange("(p t) j -> p t j", t=PACK)

        def fetch_h(c, t):
            for side, places in enumerate((list7, list8)):
                nc.vector.tensor_tensor(
                    h_fetched[c][side][:, t, :], h_win[t][:].indirect(places[:, entries(c)]), h_less_chunk[c][:, t, :], ALU.add
                )

        def finish(c):
            nc.vector.tensor_tensor(result[c][:], h_fetched[c][0][:], h_fetched[c][1][:], ALU.max)
            nc.sync.dma_start(out_rows[:, :, columns(c)], result[c][:])

        def quantise_result(c):
            nc.vector.quantize_mx(
                out=out_codes[:, columns(c)].bitcast(FP8X4), scales=out_plane[:, columns(c)], in_=result_bf[c][:]
            )

        def store_codes(queue, span):
            queue.dma_start(as_words(out_1)[:, span], out_codes[:, span].bitcast(I32))

        u, lead = h_fetched[0]
        chunk_blocks = range(width(0) // P)
        for t in range(PACK):
            nc.vector.tensor_copy(u[:, t, :], h_win[t][:].indirect(list7[:, entries(0)]))
        for t in range(PACK):
            nc.vector.tensor_tensor(lead[:, t, :], h_win[t][:].indirect(list8[:, entries(0)]), u[:, t, :], ALU.subtract)
        base, gap = {}, {}
        for jb in chunk_blocks:
            acc = bank()
            for t in range(PACK):
                add_transposed(acc[:, block(t)], h_less_chunk[0][:, t, block(jb)], u[:, t, block(jb)])
            base[jb] = sbuf(f"base{jb}", [P, S], F32)
            nc.scalar.copy(base[jb][:], acc[:])
        lead_bank = [bank() for jb in chunk_blocks]
        for t in range(PACK):
            for jb in chunk_blocks:
                nc.tensor.transpose(lead_bank[jb][:, block(t)], lead[:, t, block(jb)], identity[:])
        for jb in chunk_blocks:
            gap[jb] = sbuf(f"gap{jb}", [P, S], F32)
            nc.scalar.activation(gap[jb][:], lead_bank[jb][:], ACT.Relu)
        for jb in chunk_blocks:
            acc = bank()
            for t in range(PACK):
                add_transposed(acc[:, block(t)], base[jb][:, block(t)], gap[jb][:, block(t)])
            nc.scalar.copy(woven(result_bf[0][:, PACK * P * jb : PACK * P * (jb + 1)]), by_row(bank_rows(acc)))
            nc.scalar.copy(result[0][:, :, block(jb)], bank_rows(acc))
        nc.sync.dma_start(out_rows[:, :, columns(0)], result[0][:])

        for t in range(PACK):
            fetch_h(1, t)
        fetch_h(LAST, 0)
        finish(1)
        result_bf[1] = sbuf("result_bf1", [P, PACK * width(1)], BF16, f"gap{chunk_blocks[-1]}")
        nc.scalar.copy(woven(result_bf[1][:]), by_row(result[1][:]))

        for t in range(1, PACK):
            fetch_h(LAST, t)
        quantise_result(0)
        store_codes(nc.sync, columns(0))
        result_bf[LAST] = sbuf(f"result_bf{LAST}", [P, PACK * width(LAST)], BF16, "result_bf0")
        nc.vector.tensor_tensor(
            woven(result_bf[LAST][:]), by_row(h_fetched[LAST][0][:]), by_row(h_fetched[LAST][1][:]), ALU.max
        )
        quantise_result(1)
        finish(LAST)
        quantise_result(LAST)

        store_codes(nc.scalar, slice(HALF, S))
        for q in range(QUADRANTS):
            queue = nc.scalar if q == QUADRANTS - 1 else nc.sync
            queue.dma_start(out_2[0, 4 * q : 4 * q + 4, :].bitcast(I32), out_plane[:].bitcast(I32)[32 * q : 32 * q + 4, :])
